import numpy as np
import ml_dtypes


def mxq(x, axis, fmt="e4m3"):
    dtype, down = {"e4m3": (ml_dtypes.float8_e4m3fn, 7), "e5m2": (ml_dtypes.float8_e5m2, 14)}[fmt]
    v = np.moveaxis(np.asarray(x, np.float32).astype(ml_dtypes.bfloat16).astype(np.float64), axis, -1)
    blocks = v.reshape(v.shape[:-1] + (-1, 32))
    amax = np.abs(blocks).max(-1, keepdims=True)
    byte = np.maximum(np.where(amax > 0, np.frexp(amax)[1] - 1 + 127, 0) - down, 1)
    scale = np.exp2(byte - 127.0)
    codes = (blocks / scale).astype(np.float32).astype(dtype).astype(np.float64)
    return np.moveaxis((codes * scale).reshape(v.shape), -1, axis)


WIDE = False


def mx_kscale(k):
    if not WIDE:
        return np.ones(k)
    levels = np.array([10, -10, 5, -5, 0])
    if k % 512:
        return np.exp2(np.random.permutation(np.resize(levels, k // 32))).repeat(32)
    a = np.empty((k // 512, 16))
    for p in range(k // 512):
        a[p, :8] = np.random.permutation(np.resize(levels, 8))
        for g in range(8):
            far = levels[np.abs(levels - a[p, g]) >= 10]
            a[p, g + 8] = far[np.random.randint(len(far))]
    return np.exp2(a.ravel()).repeat(32)


def f64(x):
    return np.asarray(x).astype(np.float64)


def striped(idx):
    return np.tile(idx.reshape(-1, 16).T, (8, 1)).astype(np.uint16)


def unstriped(offs):
    return offs[:16].T.reshape(-1).astype(np.int64)


def striped8(idx):
    return np.concatenate([x.reshape(-1, 16).T for x in idx]).astype(np.uint16)


def runs(offs, k):
    lists = np.stack([offs[16 * r : 16 * r + 16].T.reshape(-1) for r in range(8)]).astype(np.int64)
    return lists[np.arange(k) % 512 // 64]


def pack_weight(w):
    k, n = w.shape
    w = f64(np.asarray(w, np.float32).astype(ml_dtypes.bfloat16)).reshape(k // 32, 32, n)
    amax = np.abs(w).max(1)
    byte = np.clip(np.where(amax > 0, np.frexp(amax)[1] - 1 + 127 - 7, 1), 1, 254)
    scaled = (w * np.exp2(127.0 - byte)[:, None, :]).reshape(k, n).astype(np.float32)
    words = np.ascontiguousarray(scaled.reshape(k // 512, 128, 4, n).transpose(0, 1, 3, 2)).astype(ml_dtypes.float8_e4m3fn).view(np.uint8)
    return words, np.ascontiguousarray(byte.astype(np.uint8).reshape(k // 512, 16, n))


def unpack_weight(words, scales):
    g, p, n, _ = words.shape
    vals = np.ascontiguousarray(words).view(ml_dtypes.float8_e4m3fn).astype(np.float64) * np.repeat(np.exp2(scales.astype(np.float64) - 127.0), 8, axis=1)[..., None]
    return vals.transpose(0, 1, 3, 2).reshape(g * 512, n)


def relu(v):
    return np.maximum(v, 0.0)


K, T, S, N, G, H, W = 512, 1024, 256, 512, 2048, 512, 128


def setup_inputs():
    n = np.random.standard_normal
    s = mx_kscale(K)[:, None]
    u = mx_kscale(K)
    packed_xT = pack_weight(n((K, T)) * s)
    packed_dT = pack_weight(n((K, G)) / s)
    perm = np.random.permutation(S)
    return {
        "x_words": packed_xT[0],
        "x_scales": packed_xT[1],
        "d_words": packed_dT[0],
        "d_scales": packed_dT[1],
        "gn": (np.random.uniform(0.5, 1.5, (H, 1)) * u[:, None]).astype(np.float32),
        "w1": (n((H, N)) / np.sqrt(H) / u[:, None]).astype(np.float32),
        "offs": striped8(np.random.randint(0, T, (8, S))),
        "ka": striped8(np.random.randint(0, G, (8, H))),
        "kb": striped8(np.random.randint(0, G, (8, H))),
        "n1": striped(perm[:W]),
        "n2": striped(perm[W:]),
        "n3": striped(np.random.permutation(S)),
    }


def reference(x_words, x_scales, d_words, d_scales, gn, w1, offs, ka, kb, n1, n2, n3):
    d_ka = unpack_weight(d_words, d_scales)[np.arange(K)[:, None], runs(ka, K)]
    xq = unpack_weight(x_words, x_scales)[np.arange(K)[:, None], runs(offs, K)]
    d_kb = unpack_weight(d_words, d_scales)[np.arange(K)[:, None], runs(kb, K)]
    h = 0.0625 * (d_ka.T @ xq + d_kb.T @ xq)
    pa = h[:, unstriped(n1)]
    pb = h[:, unstriped(n2)]
    rb = np.maximum(pa, pb)
    ra = pa / (np.abs(pb) + 0.5)
    ds = np.zeros((H, S))
    ds[:, unstriped(n1)] = ra
    dt = ds.copy()
    dt[:, unstriped(n2)] = rb
    z = f64(gn) * dt
    h2 = mxq(f64(w1), 0, "e4m3").T @ mxq(z, 0, "e4m3")
    rl = relu(h2)
    ds2 = np.zeros((N, S))
    ds2[:, unstriped(n3)] = rl
    return ds2 - (0.5 * h2)

@@ -1,0 +1,174 @@
+from contextlib import ExitStack
+
+import concourse.mybir as mybir
+
+K, T, S, N, G, H, W = 512, 1024, 256, 512, 2048, 512, 128
+FLOPS = 2 * (2 * K * H * S + H * N * S)
+
+F32 = mybir.dt.float32
+BF16 = mybir.dt.bfloat16
+I32 = mybir.dt.int32
+U32 = mybir.dt.uint32
+U16 = mybir.dt.uint16
+U8 = mybir.dt.uint8
+FP8X4 = mybir.dt.float8_e4m3fn_x4
+ALU = mybir.AluOpType
+COPY = mybir.ActivationFunctionType.Copy
+
+P = 128
+PACK = 4
+
+
+def tile_picked_haqratiosend_none_p_kernel(
+    tc, x_words, x_scales, d_words, d_scales, gn, w1, offs, ka, kb, n1, n2, n3, out
+):
+    nc = tc.nc
+    with ExitStack() as ctx:
+        keep = ctx.enter_context(tc.tile_pool(name="keep", bufs=1))
+        psum = ctx.enter_context(tc.psum_pool(name="psum", bufs=1))
+
+        def load_list(name, src):
+            lst = keep.tile(list(src.shape), U16, name=name)
+            nc.sync.dma_start(lst[:], src)
+            return lst
+
+        d_bytes = keep.tile([P, G], U8)
+        x_bytes = keep.tile([P, T], U8)
+        planes = keep.tile([P, 2 * H + S], U8, align_bytes=64)
+        nc.vector.memset(d_bytes[:].bitcast(I32), 0)
+        nc.gpsimd.memset(x_bytes[:].bitcast(I32), 0)
+        nc.gpsimd.memset(planes[:].bitcast(I32), 0)
+        nc.scalar.dma_start(d_bytes[0:P:8, :].bitcast(I32), d_scales[0].bitcast(I32))
+        nc.scalar.dma_start(x_bytes[0:P:8, :].bitcast(I32), x_scales[0].bitcast(I32))
+
+        ka_l = load_list("ka_l", ka)
+        kb_l = load_list("kb_l", kb)
+        offs_l = load_list("offs_l", offs)
+        x_tab = keep.tile([P, T], I32)
+        d_tab = keep.tile([P, G], I32)
+        nc.sync.dma_start(x_tab[:], x_words[0].rearrange("p n t -> p (n t)").bitcast(I32))
+        nc.sync.dma_start(d_tab[:], d_words[0].rearrange("p n t -> p (n t)").bitcast(I32))
+        n1_l = load_list("n1_l", n1)
+        n2_l = load_list("n2_l", n2)
+        w_raw = []
+        for half in range(2):
+            raw = keep.tile([P, PACK, N // 2], F32, name="w_raw%d" % half)
+            nc.sync.dma_start(raw[:], w1.rearrange("(p j) n -> p j n", j=PACK)[:, :, half * 256 : (half + 1) * 256])
+            w_raw.append(raw)
+        gain = keep.tile([P, PACK], F32)
+        nc.sync.dma_start(gain[:], gn.rearrange("(p j) o -> p (j o)", j=PACK))
+        n3_l = load_list("n3_l", n3)
+
+        dealt_bytes = keep.tile([P, 2 * H + S], U8)
+        picked_bytes = []
+        for name, table, lst, width in (("a", d_bytes, ka_l, H), ("b", d_bytes, kb_l, H), ("x", x_bytes, offs_l, S)):
+            picked = keep.tile([P, width], U8, name="bytes_" + name, tag="picked_" + name, align_bytes=64)
+            nc.vector.tensor_copy(picked[:], table[:].indirect(lst[:]))
+            picked_bytes.append(picked)
+        for li in range(2):
+            nc.vector.tensor_copy(
+                dealt_bytes[:, li * H : (li + 1) * H].rearrange("p (t m) -> p m t", t=PACK),
+                picked_bytes[li][:].rearrange("p (m t) -> p m t", t=PACK),
+            )
+        nc.vector.tensor_copy(dealt_bytes[:, 2 * H :].bitcast(I32), picked_bytes[2][:].bitcast(I32))
+        for b in range(4):
+            nc.sync.dma_start(planes[b:P:32, :].bitcast(I32), dealt_bytes[8 * b : P : 32, :].bitcast(I32))
+
+        x_codes = keep.tile([P, S], U32, tag="picked_x", align_bytes=64)
+        nc.vector.tensor_copy(x_codes[:], x_tab[:].bitcast(U32).indirect(offs_l[:]))
+        picked_words = []
+        for name, lst in (("a", ka_l), ("b", kb_l)):
+            picked = keep.tile([P, H], U32, name="words_" + name, tag="picked_" + name, align_bytes=64)
+            nc.vector.tensor_copy(picked[:], d_tab[:].bitcast(U32).indirect(lst[:]))
+            picked_words.append(picked)
+        d_codes = []
+        for li in range(2):
+            dealt = keep.tile([P, H], U32, name="d_codes%d" % li, align_bytes=64)
+            nc.vector.tensor_copy(
+                dealt[:].rearrange("p (t m) -> p m t", t=PACK),
+                picked_words[li][:].rearrange("p (m t) -> p m t", t=PACK),
+            )
+            d_codes.append(dealt)
+
+        w_grouped = []
+        for mt in range(4):
+            grouped = keep.tile([P, P, PACK], BF16, name="w_grouped%d" % mt, align_bytes=64)
+            cols = slice((mt % 2) * P, (mt % 2 + 1) * P)
+            nc.scalar.copy(
+                grouped[:].rearrange("p (c i) j -> p c j i", i=4),
+                w_raw[mt // 2][:, :, cols].rearrange("p j (c i) -> p c j i", i=4),
+            )
+            w_grouped.append(grouped)
+
+        w_mx = []
+        for mt in range(4):
+            codes = keep.tile([P, P], U32, name="w_codes%d" % mt, align_bytes=64)
+            scales = keep.tile([P, P], U8, name="w_scales%d" % mt, align_bytes=64)
+            nc.vector.quantize_mx(codes[:].bitcast(FP8X4), scales[:], w_grouped[mt][:].rearrange("p c j -> p (c j)"))
+            w_mx.append((codes, scales))
+
+        h_ps = [psum.tile([P, S], F32, name="h_ps%d" % t) for t in range(PACK)]
+        for li in range(2):
+            for t in range(PACK):
+                nc.tensor.matmul_mx(
+                    out=h_ps[t][:],
+                    lhsT=d_codes[li][:, t * P : (t + 1) * P].bitcast(FP8X4),
+                    lhsT_scale=planes[:, li * H + t * P : li * H + (t + 1) * P],
+                    rhs=x_codes[:].bitcast(FP8X4),
+                    rhs_scale=planes[:, 2 * H :],
+                    start=(li == 0),
+                    stop=(li == 1),
+                )
+
+        dts = []
+        for t in range(PACK):
+            h = keep.tile([P, S], F32, name="h%d" % t)
+            if t == 0:
+                nc.scalar.activation(h[:], h_ps[t][:], COPY, scale=0.0625)
+            else:
+                nc.vector.tensor_scalar(h[:], h_ps[t][:], 0.0625, None, ALU.mult)
+            pa = keep.tile([P, W], F32, name="pa%d" % t)
+            pb = keep.tile([P, W], F32, name="pb%d" % t)
+            nc.scalar.activation(pb[:], h[:].indirect(n2_l[:]), COPY)
+            nc.scalar.activation(pa[:], h[:].indirect(n1_l[:]), COPY)
+            flipped = keep.tile([P, W], F32, name="flipped%d" % t)
+            den = keep.tile([P, W], F32, name="den%d" % t)
+            rec = keep.tile([P, W], F32, name="rec%d" % t, align_bytes=64)
+            ra = keep.tile([P, W], F32, name="ra%d" % t)
+            rb = keep.tile([P, W], F32, name="rb%d" % t)
+            nc.vector.tensor_scalar(flipped[:], pb[:], -1.0, 0.5, ALU.mult, ALU.add)
+            nc.vector.tensor_tensor(rb[:], pa[:], pb[:], ALU.max)
+            nc.vector.scalar_tensor_tensor(den[:], pb[:], 0.5, flipped[:], ALU.add, ALU.max)
+            nc.vector.reciprocal(rec[:], den[:])
+            nc.vector.tensor_tensor(ra[:], pa[:], rec[:], ALU.mult)
+            dt = keep.tile([P, S], F32, name="dt%d" % t)
+            nc.scalar.activation(dt[:].indirect(n2_l[:]), rb[:], COPY)
+            nc.scalar.activation(dt[:].indirect(n1_l[:]), ra[:], COPY)
+            dts.append(dt)
+
+        z = keep.tile([P, S, PACK], BF16, tag="rec3", align_bytes=64)
+        for t in range(PACK):
+            nc.vector.tensor_scalar(z[:, :, t], dts[t][:], gain[:, t : t + 1], None, ALU.mult)
+
+        z_codes = keep.tile([P, S], U32, align_bytes=64)
+        z_scales = keep.tile([P, S], U8, align_bytes=64)
+        nc.vector.quantize_mx(z_codes[:].bitcast(FP8X4), z_scales[:], z[:].rearrange("p c j -> p (c j)"))
+
+        for mt in range(4):
+            h2 = psum.tile([P, S], F32, name="h2_ps%d" % mt)
+            nc.tensor.matmul_mx(
+                out=h2[:],
+                lhsT=w_mx[mt][0][:].bitcast(FP8X4),
+                lhsT_scale=w_mx[mt][1][:],
+                rhs=z_codes[:].bitcast(FP8X4),
+                rhs_scale=z_scales[:],
+                start=True,
+                stop=True,
+            )
+            rl = keep.tile([P, S], F32, name="rl%d" % mt)
+            nc.vector.tensor_scalar(rl[:], h2[:], 0.0, None, ALU.max)
+            sent = keep.tile([P, 2 * S], F32, name="sent%d" % mt)
+            nc.scalar.activation(sent[:].indirect(n3_l[:]), rl[:], COPY)
+            res = keep.tile([P, S], F32, name="res%d" % mt)
+            nc.vector.scalar_tensor_tensor(res[:], h2[:], -0.5, sent[:, 0:S], ALU.mult, ALU.add)
+            nc.sync.dma_start(out[mt * P : (mt + 1) * P, :], res[:])

@@ -32,14 +32,14 @@ def tile_picked_haqratiosend_none_p_kernel(
             nc.sync.dma_start(lst[:], src)
             return lst
 
-        d_bytes = keep.tile([P, G], U8)
-        x_bytes = keep.tile([P, T], U8)
-        planes = keep.tile([P, 2 * H + S], U8, align_bytes=64)
+        d_bytes = keep.tile([P, G], U8, tag="d_stage", align_bytes=64)
+        x_bytes = keep.tile([P, T], U8, tag="x_stage", align_bytes=64)
+        moved = keep.tile([P, 2 * H + S], U8, align_bytes=64)
         nc.vector.memset(d_bytes[:].bitcast(I32), 0)
         nc.gpsimd.memset(x_bytes[:].bitcast(I32), 0)
-        nc.gpsimd.memset(planes[:].bitcast(I32), 0)
-        nc.scalar.dma_start(d_bytes[0:P:8, :].bitcast(I32), d_scales[0].bitcast(I32))
-        nc.scalar.dma_start(x_bytes[0:P:8, :].bitcast(I32), x_scales[0].bitcast(I32))
+        nc.gpsimd.memset(moved[:].bitcast(I32), 0)
+        nc.sync.dma_start(d_bytes[0:P:8, :].bitcast(I32), d_scales[0].bitcast(I32))
+        nc.sync.dma_start(x_bytes[0:P:8, :].bitcast(I32), x_scales[0].bitcast(I32))
 
         ka_l = load_list("ka_l", ka)
         kb_l = load_list("kb_l", kb)
@@ -47,75 +47,66 @@ def tile_picked_haqratiosend_none_p_kernel(
         x_tab = keep.tile([P, T], I32)
         d_tab = keep.tile([P, G], I32)
         nc.sync.dma_start(x_tab[:], x_words[0].rearrange("p n t -> p (n t)").bitcast(I32))
-        nc.sync.dma_start(d_tab[:], d_words[0].rearrange("p n t -> p (n t)").bitcast(I32))
-        n1_l = load_list("n1_l", n1)
         n2_l = load_list("n2_l", n2)
-        w_raw = []
-        for half in range(2):
-            raw = keep.tile([P, PACK, N // 2], F32, name="w_raw%d" % half)
-            nc.sync.dma_start(raw[:], w1.rearrange("(p j) n -> p j n", j=PACK)[:, :, half * 256 : (half + 1) * 256])
-            w_raw.append(raw)
+        n1_l = load_list("n1_l", n1)
+        nc.sync.dma_start(d_tab[:], d_words[0].rearrange("p n t -> p (n t)").bitcast(I32))
+        w_rows = w1.rearrange("(p j) n -> p j n", j=PACK)
+        w_raw0 = keep.tile([P, PACK, N // 2], F32)
+        nc.sync.dma_start(w_raw0[:], w_rows[:, :, 0 : N // 2])
         gain = keep.tile([P, PACK], F32)
-        nc.sync.dma_start(gain[:], gn.rearrange("(p j) o -> p (j o)", j=PACK))
+        nc.scalar.dma_start(gain[:], gn.rearrange("(p j) o -> p (j o)", j=PACK))
         n3_l = load_list("n3_l", n3)
 
-        dealt_bytes = keep.tile([P, 2 * H + S], U8)
-        picked_bytes = []
-        for name, table, lst, width in (("a", d_bytes, ka_l, H), ("b", d_bytes, kb_l, H), ("x", x_bytes, offs_l, S)):
-            picked = keep.tile([P, width], U8, name="bytes_" + name, tag="picked_" + name, align_bytes=64)
-            nc.vector.tensor_copy(picked[:], table[:].indirect(lst[:]))
-            picked_bytes.append(picked)
-        for li in range(2):
-            nc.vector.tensor_copy(
-                dealt_bytes[:, li * H : (li + 1) * H].rearrange("p (t m) -> p m t", t=PACK),
-                picked_bytes[li][:].rearrange("p (m t) -> p m t", t=PACK),
-            )
-        nc.vector.tensor_copy(dealt_bytes[:, 2 * H :].bitcast(I32), picked_bytes[2][:].bitcast(I32))
+        picked_bytes = keep.tile([P, 2 * H + S], U8, tag="late_w")
+        nc.vector.tensor_copy(picked_bytes[:, 0:H], d_bytes[:].indirect(ka_l[:]))
+        nc.vector.tensor_copy(picked_bytes[:, H : 2 * H], d_bytes[:].indirect(kb_l[:]))
+        nc.vector.tensor_copy(picked_bytes[:, 2 * H :], x_bytes[:].indirect(offs_l[:]))
         for b in range(4):
-            nc.sync.dma_start(planes[b:P:32, :].bitcast(I32), dealt_bytes[8 * b : P : 32, :].bitcast(I32))
+            nc.scalar.dma_start(moved[b:P:32, :].bitcast(I32), picked_bytes[8 * b : P : 32, :].bitcast(I32))
 
-        x_codes = keep.tile([P, S], U32, tag="picked_x", align_bytes=64)
+        w_raw1 = keep.tile([P, PACK, N // 2], F32, tag="late_w")
+        nc.sync.dma_start(w_raw1[:], w_rows[:, :, N // 2 : N])
+        w_raw = [w_raw0, w_raw1]
+
+        x_codes = keep.tile([P, S], U32, tag="x_stage", align_bytes=64)
         nc.vector.tensor_copy(x_codes[:], x_tab[:].bitcast(U32).indirect(offs_l[:]))
-        picked_words = []
-        for name, lst in (("a", ka_l), ("b", kb_l)):
-            picked = keep.tile([P, H], U32, name="words_" + name, tag="picked_" + name, align_bytes=64)
-            nc.vector.tensor_copy(picked[:], d_tab[:].bitcast(U32).indirect(lst[:]))
-            picked_words.append(picked)
-        d_codes = []
-        for li in range(2):
-            dealt = keep.tile([P, H], U32, name="d_codes%d" % li, align_bytes=64)
-            nc.vector.tensor_copy(
-                dealt[:].rearrange("p (t m) -> p m t", t=PACK),
-                picked_words[li][:].rearrange("p (m t) -> p m t", t=PACK),
-            )
-            d_codes.append(dealt)
+        picked_words = keep.tile([P, 2 * H], U32, tag="d_stage", align_bytes=64)
+        nc.vector.tensor_copy(picked_words[:, 0:H], d_tab[:].bitcast(U32).indirect(ka_l[:]))
+        nc.vector.tensor_copy(picked_words[:, H : 2 * H], d_tab[:].bitcast(U32).indirect(kb_l[:]))
+        d_mx = []
+        for t in range(PACK):
+            codes = keep.tile([P, 2 * P], U32, name="d_codes%d" % t, align_bytes=64)
+            scales = keep.tile([P, 2 * P], U8, name="d_planes%d" % t, align_bytes=64)
+            nc.vector.tensor_copy(scales[:], moved[:, t : 2 * H : PACK])
+            nc.vector.tensor_copy(codes[:], picked_words[:, t : 2 * H : PACK])
+            d_mx.append((codes, scales))
 
-        w_grouped = []
-        for mt in range(4):
-            grouped = keep.tile([P, P, PACK], BF16, name="w_grouped%d" % mt, align_bytes=64)
+        def interleave_w(mt, copy, tag):
+            grouped = keep.tile([P, P, PACK], BF16, name="w_grouped%d" % mt, tag=tag, align_bytes=64)
             cols = slice((mt % 2) * P, (mt % 2 + 1) * P)
-            nc.scalar.copy(
+            copy(
                 grouped[:].rearrange("p (c i) j -> p c j i", i=4),
                 w_raw[mt // 2][:, :, cols].rearrange("p j (c i) -> p c j i", i=4),
             )
-            w_grouped.append(grouped)
+            return grouped
 
-        w_mx = []
-        for mt in range(4):
-            codes = keep.tile([P, P], U32, name="w_codes%d" % mt, align_bytes=64)
+        def quantize_w(mt, grouped):
+            codes = keep.tile([P, P], U32, name="w_codes%d" % mt, tag="d_codes%d" % mt, align_bytes=64)
             scales = keep.tile([P, P], U8, name="w_scales%d" % mt, align_bytes=64)
-            nc.vector.quantize_mx(codes[:].bitcast(FP8X4), scales[:], w_grouped[mt][:].rearrange("p c j -> p (c j)"))
-            w_mx.append((codes, scales))
+            nc.vector.quantize_mx(codes[:].bitcast(FP8X4), scales[:], grouped[:].rearrange("p c j -> p (c j)"))
+            return codes, scales
+
+        w_mx = [quantize_w(mt, interleave_w(mt, nc.scalar.copy, "w_grouped%d" % mt)) for mt in range(2)]
 
         h_ps = [psum.tile([P, S], F32, name="h_ps%d" % t) for t in range(PACK)]
-        for li in range(2):
-            for t in range(PACK):
+        for t in range(PACK):
+            for li in range(2):
                 nc.tensor.matmul_mx(
                     out=h_ps[t][:],
-                    lhsT=d_codes[li][:, t * P : (t + 1) * P].bitcast(FP8X4),
-                    lhsT_scale=planes[:, li * H + t * P : li * H + (t + 1) * P],
+                    lhsT=d_mx[t][0][:, li * P : (li + 1) * P].bitcast(FP8X4),
+                    lhsT_scale=d_mx[t][1][:, li * P : (li + 1) * P],
                     rhs=x_codes[:].bitcast(FP8X4),
-                    rhs_scale=planes[:, 2 * H :],
+                    rhs_scale=moved[:, 2 * H :],
                     start=(li == 0),
                     stop=(li == 1),
                 )
@@ -154,7 +145,7 @@ def tile_picked_haqratiosend_none_p_kernel(
         z_scales = keep.tile([P, S], U8, align_bytes=64)
         nc.vector.quantize_mx(z_codes[:].bitcast(FP8X4), z_scales[:], z[:].rearrange("p c j -> p (c j)"))
 
-        for mt in range(4):
+        def product(mt):
             h2 = psum.tile([P, S], F32, name="h2_ps%d" % mt)
             nc.tensor.matmul_mx(
                 out=h2[:],
@@ -165,10 +156,22 @@ def tile_picked_haqratiosend_none_p_kernel(
                 start=True,
                 stop=True,
             )
+            return h2
+
+        def send(mt, h2):
             rl = keep.tile([P, S], F32, name="rl%d" % mt)
             nc.vector.tensor_scalar(rl[:], h2[:], 0.0, None, ALU.max)
             sent = keep.tile([P, 2 * S], F32, name="sent%d" % mt)
             nc.scalar.activation(sent[:].indirect(n3_l[:]), rl[:], COPY)
-            res = keep.tile([P, S], F32, name="res%d" % mt)
-            nc.vector.scalar_tensor_tensor(res[:], h2[:], -0.5, sent[:, 0:S], ALU.mult, ALU.add)
+            return sent
+
+        h2s = [product(mt) for mt in range(2)]
+        sents = [send(mt, h2s[mt]) for mt in range(2)]
+        for mt in range(2, 4):
+            w_mx.append(quantize_w(mt, interleave_w(mt, nc.vector.tensor_copy, "w_scales%d" % (mt - 2))))
+            h2s.append(product(mt))
+        sents.extend([send(mt, h2s[mt]) for mt in range(2, 4)])
+        for mt in range(4):
+            res = keep.tile([P, S], F32, name="res%d" % mt, tag="d_codes3" if mt == 1 else "res%d" % mt, align_bytes=64)
+            nc.vector.scalar_tensor_tensor(res[:], h2s[mt][:], -0.5, sents[mt][:, 0:S], ALU.mult, ALU.add)
             nc.sync.dma_start(out[mt * P : (mt + 1) * P, :], res[:])

@@ -35,17 +35,16 @@ def tile_picked_haqratiosend_none_p_kernel(
         d_bytes = keep.tile([P, G], U8, tag="d_stage", align_bytes=64)
         x_bytes = keep.tile([P, T], U8, tag="x_stage", align_bytes=64)
         moved = keep.tile([P, 2 * H + S], U8, align_bytes=64)
+        nc.vector.memset(x_bytes[:].bitcast(I32), 0)
         nc.vector.memset(d_bytes[:].bitcast(I32), 0)
-        nc.gpsimd.memset(x_bytes[:].bitcast(I32), 0)
         nc.gpsimd.memset(moved[:].bitcast(I32), 0)
-        nc.sync.dma_start(d_bytes[0:P:8, :].bitcast(I32), d_scales[0].bitcast(I32))
-        nc.sync.dma_start(x_bytes[0:P:8, :].bitcast(I32), x_scales[0].bitcast(I32))
-
-        ka_l = load_list("ka_l", ka)
-        kb_l = load_list("kb_l", kb)
         offs_l = load_list("offs_l", offs)
+        nc.sync.dma_start(x_bytes[0:P:8, :].bitcast(I32), x_scales[0].bitcast(I32))
+        ka_l = load_list("ka_l", ka)
+        nc.sync.dma_start(d_bytes[0:P:8, :].bitcast(I32), d_scales[0].bitcast(I32))
+        kb_l = load_list("kb_l", kb)
         x_tab = keep.tile([P, T], I32)
-        d_tab = keep.tile([P, G], I32)
+        d_tab = keep.tile([P, G], I32, tag="d_table", align_bytes=64)
         nc.sync.dma_start(x_tab[:], x_words[0].rearrange("p n t -> p (n t)").bitcast(I32))
         n2_l = load_list("n2_l", n2)
         n1_l = load_list("n1_l", n1)
@@ -58,9 +57,9 @@ def tile_picked_haqratiosend_none_p_kernel(
         n3_l = load_list("n3_l", n3)
 
         picked_bytes = keep.tile([P, 2 * H + S], U8, tag="late_w")
+        nc.vector.tensor_copy(picked_bytes[:, 2 * H :], x_bytes[:].indirect(offs_l[:]))
         nc.vector.tensor_copy(picked_bytes[:, 0:H], d_bytes[:].indirect(ka_l[:]))
         nc.vector.tensor_copy(picked_bytes[:, H : 2 * H], d_bytes[:].indirect(kb_l[:]))
-        nc.vector.tensor_copy(picked_bytes[:, 2 * H :], x_bytes[:].indirect(offs_l[:]))
         for b in range(4):
             nc.scalar.dma_start(moved[b:P:32, :].bitcast(I32), picked_bytes[8 * b : P : 32, :].bitcast(I32))
 
@@ -68,16 +67,17 @@ def tile_picked_haqratiosend_none_p_kernel(
         nc.sync.dma_start(w_raw1[:], w_rows[:, :, N // 2 : N])
         w_raw = [w_raw0, w_raw1]
 
-        x_codes = keep.tile([P, S], U32, tag="x_stage", align_bytes=64)
+        x_codes = keep.tile([P, S], U32, tag="d_stage", align_bytes=64)
         nc.vector.tensor_copy(x_codes[:], x_tab[:].bitcast(U32).indirect(offs_l[:]))
-        picked_words = keep.tile([P, 2 * H], U32, tag="d_stage", align_bytes=64)
+        picked_words = keep.tile([P, 2 * H], U32, tag="x_stage", align_bytes=64)
         nc.vector.tensor_copy(picked_words[:, 0:H], d_tab[:].bitcast(U32).indirect(ka_l[:]))
         nc.vector.tensor_copy(picked_words[:, H : 2 * H], d_tab[:].bitcast(U32).indirect(kb_l[:]))
+        d_planes = keep.tile([P, PACK, 2 * P], U8, tag="d_table", align_bytes=64)
         d_mx = []
         for t in range(PACK):
             codes = keep.tile([P, 2 * P], U32, name="d_codes%d" % t, align_bytes=64)
-            scales = keep.tile([P, 2 * P], U8, name="d_planes%d" % t, align_bytes=64)
-            nc.vector.tensor_copy(scales[:], moved[:, t : 2 * H : PACK])
+            scales = d_planes[:, t, :]
+            nc.vector.tensor_copy(scales, moved[:, t : 2 * H : PACK])
             nc.vector.tensor_copy(codes[:], picked_words[:, t : 2 * H : PACK])
             d_mx.append((codes, scales))
 
@@ -90,13 +90,13 @@ def tile_picked_haqratiosend_none_p_kernel(
             )
             return grouped
 
-        def quantize_w(mt, grouped):
-            codes = keep.tile([P, P], U32, name="w_codes%d" % mt, tag="d_codes%d" % mt, align_bytes=64)
+        def quantize_w(mt, grouped, tag):
+            codes = keep.tile([P, P], U32, name="w_codes%d" % mt, tag=tag, align_bytes=64)
             scales = keep.tile([P, P], U8, name="w_scales%d" % mt, align_bytes=64)
             nc.vector.quantize_mx(codes[:].bitcast(FP8X4), scales[:], grouped[:].rearrange("p c j -> p (c j)"))
             return codes, scales
 
-        w_mx = [quantize_w(mt, interleave_w(mt, nc.scalar.copy, "w_grouped%d" % mt)) for mt in range(2)]
+        w_early = [interleave_w(mt, nc.scalar.copy, "w_grouped%d" % mt) for mt in range(2)]
 
         h_ps = [psum.tile([P, S], F32, name="h_ps%d" % t) for t in range(PACK)]
         for t in range(PACK):
@@ -137,41 +137,58 @@ def tile_picked_haqratiosend_none_p_kernel(
             nc.scalar.activation(dt[:].indirect(n1_l[:]), ra[:], COPY)
             dts.append(dt)
 
-        z = keep.tile([P, S, PACK], BF16, tag="rec3", align_bytes=64)
-        for t in range(PACK):
-            nc.vector.tensor_scalar(z[:, :, t], dts[t][:], gain[:, t : t + 1], None, ALU.mult)
+        w_mx = [quantize_w(mt, w_early[mt], "rec%d" % mt) for mt in range(2)]
 
+        HALF = S // 2
+        z = keep.tile([P, S, PACK], BF16, tag="rec3", align_bytes=64)
+        for t in range(PACK - 1):
+            nc.vector.tensor_scalar(z[:, :, t], dts[t][:], gain[:, t : t + 1], None, ALU.mult)
+        t = PACK - 1
+        for c0 in (0, HALF):
+            nc.vector.tensor_scalar(z[:, c0 : c0 + HALF, t], dts[t][:, c0 : c0 + HALF], gain[:, t : t + 1], None, ALU.mult)
         z_codes = keep.tile([P, S], U32, align_bytes=64)
         z_scales = keep.tile([P, S], U8, align_bytes=64)
-        nc.vector.quantize_mx(z_codes[:].bitcast(FP8X4), z_scales[:], z[:].rearrange("p c j -> p (c j)"))
+        for c0 in (0, HALF):
+            nc.vector.quantize_mx(
+                z_codes[:, c0 : c0 + HALF].bitcast(FP8X4),
+                z_scales[:, c0 : c0 + HALF],
+                z[:, c0 : c0 + HALF, :].rearrange("p c j -> p (c j)"),
+            )
 
-        def product(mt):
-            h2 = psum.tile([P, S], F32, name="h2_ps%d" % mt)
+        def product(mt, c0, width, bank):
+            h2 = psum.tile([P, width], F32, name="h2_ps%d_%d" % (mt, c0), tag=bank)
             nc.tensor.matmul_mx(
                 out=h2[:],
                 lhsT=w_mx[mt][0][:].bitcast(FP8X4),
                 lhsT_scale=w_mx[mt][1][:],
-                rhs=z_codes[:].bitcast(FP8X4),
-                rhs_scale=z_scales[:],
+                rhs=z_codes[:, c0 : c0 + width].bitcast(FP8X4),
+                rhs_scale=z_scales[:, c0 : c0 + width],
                 start=True,
                 stop=True,
             )
             return h2
 
-        def send(mt, h2):
-            rl = keep.tile([P, S], F32, name="rl%d" % mt)
+        def send(mt, c0, h2, sent):
+            width = h2.shape[1]
+            rl = keep.tile([P, width], F32, name="rl%d_%d" % (mt, c0))
             nc.vector.tensor_scalar(rl[:], h2[:], 0.0, None, ALU.max)
-            sent = keep.tile([P, 2 * S], F32, name="sent%d" % mt)
-            nc.scalar.activation(sent[:].indirect(n3_l[:]), rl[:], COPY)
-            return sent
+            nc.scalar.activation(sent[:].indirect(n3_l[:, c0 // 16 : (c0 + width) // 16]), rl[:], COPY)
 
-        h2s = [product(mt) for mt in range(2)]
-        sents = [send(mt, h2s[mt]) for mt in range(2)]
+        sents = [keep.tile([P, 2 * S], F32, name="sent%d" % mt) for mt in range(4)]
+        pieces = [[] for mt in range(4)]
+        for c0 in (0, HALF):
+            for mt in range(2):
+                h2 = product(mt, c0, HALF, "h_ps%d" % (2 * mt + c0 // HALF))
+                send(mt, c0, h2, sents[mt])
+                pieces[mt].append((c0, h2))
         for mt in range(2, 4):
-            w_mx.append(quantize_w(mt, interleave_w(mt, nc.vector.tensor_copy, "w_scales%d" % (mt - 2))))
-            h2s.append(product(mt))
-        sents.extend([send(mt, h2s[mt]) for mt in range(2, 4)])
+            w_mx.append(quantize_w(mt, interleave_w(mt, nc.vector.tensor_copy, "w_scales%d" % (mt - 2)), "d_codes%d" % mt))
+            pieces[mt].append((0, product(mt, 0, S, "h2_ps%d" % mt)))
+        for mt in range(2, 4):
+            send(mt, 0, pieces[mt][0][1], sents[mt])
         for mt in range(4):
-            res = keep.tile([P, S], F32, name="res%d" % mt, tag="d_codes3" if mt == 1 else "res%d" % mt, align_bytes=64)
-            nc.vector.scalar_tensor_tensor(res[:], h2s[mt][:], -0.5, sents[mt][:, 0:S], ALU.mult, ALU.add)
+            res = keep.tile([P, S], F32, name="res%d" % mt, tag="d_codes%d" % (mt + 2) if mt < 2 else "res%d" % mt, align_bytes=64)
+            for c0, h2 in pieces[mt]:
+                cols = slice(c0, c0 + h2.shape[1])
+                nc.vector.scalar_tensor_tensor(res[:, cols], h2[:], -0.5, sents[mt][:, cols], ALU.mult, ALU.add)
             nc.sync.dma_start(out[mt * P : (mt + 1) * P, :], res[:])

@@ -17,6 +17,13 @@ COPY = mybir.ActivationFunctionType.Copy
 
 P = 128
 PACK = 4
+BLOCK_ROWS = 8
+QUADRANT = 32
+LIST_ROWS = 16
+MX_ALIGN = 64
+OUT_TILES = N // P
+EARLY_TILES = 2
+PIECES = ((0, 64), (64, 64), (128, 128))
 
 
 def tile_picked_haqratiosend_none_p_kernel(
@@ -32,81 +39,89 @@ def tile_picked_haqratiosend_none_p_kernel(
             nc.sync.dma_start(lst[:], src)
             return lst
 
-        d_bytes = keep.tile([P, G], U8, tag="d_stage", align_bytes=64)
-        x_bytes = keep.tile([P, T], U8, tag="x_stage", align_bytes=64)
-        moved = keep.tile([P, 2 * H + S], U8, align_bytes=64)
+        d_bytes = keep.tile([P, G], U8, align_bytes=MX_ALIGN)
+        x_bytes = keep.tile([P, T], U8, tag="x_bytes", align_bytes=MX_ALIGN)
+        placed_bytes = keep.tile([P, 2 * H + S], U8, align_bytes=MX_ALIGN)
         nc.vector.memset(x_bytes[:].bitcast(I32), 0)
         nc.vector.memset(d_bytes[:].bitcast(I32), 0)
-        nc.gpsimd.memset(moved[:].bitcast(I32), 0)
+        nc.gpsimd.memset(placed_bytes[:].bitcast(I32), 0)
         offs_l = load_list("offs_l", offs)
-        nc.sync.dma_start(x_bytes[0:P:8, :].bitcast(I32), x_scales[0].bitcast(I32))
+        nc.sync.dma_start(x_bytes[0:P:BLOCK_ROWS, :].bitcast(I32), x_scales[0].bitcast(I32))
         ka_l = load_list("ka_l", ka)
-        nc.sync.dma_start(d_bytes[0:P:8, :].bitcast(I32), d_scales[0].bitcast(I32))
+        nc.sync.dma_start(d_bytes[0:P:BLOCK_ROWS, :].bitcast(I32), d_scales[0].bitcast(I32))
         kb_l = load_list("kb_l", kb)
-        x_tab = keep.tile([P, T], I32)
-        d_tab = keep.tile([P, G], I32, tag="d_table", align_bytes=64)
-        nc.sync.dma_start(x_tab[:], x_words[0].rearrange("p n t -> p (n t)").bitcast(I32))
+        x_table = keep.tile([P, T], I32)
+        d_table = keep.tile([P, G], I32, tag="d_table", align_bytes=MX_ALIGN)
+        nc.sync.dma_start(x_table[:], x_words[0].rearrange("p n t -> p (n t)").bitcast(I32))
         n2_l = load_list("n2_l", n2)
         n1_l = load_list("n1_l", n1)
-        nc.sync.dma_start(d_tab[:], d_words[0].rearrange("p n t -> p (n t)").bitcast(I32))
+        nc.sync.dma_start(d_table[:], d_words[0].rearrange("p n t -> p (n t)").bitcast(I32))
         w_rows = w1.rearrange("(p j) n -> p j n", j=PACK)
-        w_raw0 = keep.tile([P, PACK, N // 2], F32)
-        nc.sync.dma_start(w_raw0[:], w_rows[:, :, 0 : N // 2])
+        w_first = keep.tile([P, PACK, N // 2], F32)
+        nc.sync.dma_start(w_first[:], w_rows[:, :, 0 : N // 2])
         gain = keep.tile([P, PACK], F32)
         nc.scalar.dma_start(gain[:], gn.rearrange("(p j) o -> p (j o)", j=PACK))
         n3_l = load_list("n3_l", n3)
 
-        picked_bytes = keep.tile([P, 2 * H + S], U8, tag="late_w")
+        picked_bytes = keep.tile([P, 2 * H + S], U8, tag="picked_bytes")
         nc.vector.tensor_copy(picked_bytes[:, 2 * H :], x_bytes[:].indirect(offs_l[:]))
         nc.vector.tensor_copy(picked_bytes[:, 0:H], d_bytes[:].indirect(ka_l[:]))
         nc.vector.tensor_copy(picked_bytes[:, H : 2 * H], d_bytes[:].indirect(kb_l[:]))
-        for b in range(4):
-            nc.scalar.dma_start(moved[b:P:32, :].bitcast(I32), picked_bytes[8 * b : P : 32, :].bitcast(I32))
+        for b in range(QUADRANT // BLOCK_ROWS):
+            nc.scalar.dma_start(
+                placed_bytes[b:P:QUADRANT, :].bitcast(I32),
+                picked_bytes[BLOCK_ROWS * b : P : QUADRANT, :].bitcast(I32),
+            )
 
-        w_raw1 = keep.tile([P, PACK, N // 2], F32, tag="late_w")
-        nc.sync.dma_start(w_raw1[:], w_rows[:, :, N // 2 : N])
-        w_raw = [w_raw0, w_raw1]
+        w_second = keep.tile([P, PACK, N // 2], F32, tag="picked_bytes")
+        nc.sync.dma_start(w_second[:], w_rows[:, :, N // 2 : N])
+        w_halves = [w_first, w_second]
 
-        x_codes = keep.tile([P, S], U32, tag="d_stage", align_bytes=64)
-        nc.vector.tensor_copy(x_codes[:], x_tab[:].bitcast(U32).indirect(offs_l[:]))
-        picked_words = keep.tile([P, 2 * H], U32, tag="x_stage", align_bytes=64)
-        nc.vector.tensor_copy(picked_words[:, 0:H], d_tab[:].bitcast(U32).indirect(ka_l[:]))
-        nc.vector.tensor_copy(picked_words[:, H : 2 * H], d_tab[:].bitcast(U32).indirect(kb_l[:]))
-        d_planes = keep.tile([P, PACK, 2 * P], U8, tag="d_table", align_bytes=64)
-        d_mx = []
+        x_codes = keep.tile([P, S], U32, align_bytes=MX_ALIGN)
+        nc.vector.tensor_copy(x_codes[:], x_table[:].bitcast(U32).indirect(offs_l[:]))
+        picked_words = keep.tile([P, 2 * H], U32, tag="x_bytes", align_bytes=MX_ALIGN)
+        nc.vector.tensor_copy(picked_words[:, 0:H], d_table[:].bitcast(U32).indirect(ka_l[:]))
+        nc.vector.tensor_copy(picked_words[:, H : 2 * H], d_table[:].bitcast(U32).indirect(kb_l[:]))
+
+        d_planes = keep.tile([P, PACK, 2 * P], U8, tag="d_table", align_bytes=MX_ALIGN)
+        d_codes = []
         for t in range(PACK):
-            codes = keep.tile([P, 2 * P], U32, name="d_codes%d" % t, align_bytes=64)
-            scales = d_planes[:, t, :]
-            nc.vector.tensor_copy(scales, moved[:, t : 2 * H : PACK])
-            nc.vector.tensor_copy(codes[:], picked_words[:, t : 2 * H : PACK])
-            d_mx.append((codes, scales))
+            codes = keep.tile([P, 2 * P], U32, name="d_codes%d" % t, align_bytes=MX_ALIGN)
+            if t == 0:
+                nc.vector.tensor_copy(codes[:, 0:P], picked_words[:, 0:H:PACK])
+                nc.vector.tensor_copy(d_planes[:, t, :], placed_bytes[:, t : 2 * H : PACK])
+                nc.vector.tensor_copy(codes[:, P : 2 * P], picked_words[:, H : 2 * H : PACK])
+            else:
+                nc.vector.tensor_copy(d_planes[:, t, :], placed_bytes[:, t : 2 * H : PACK])
+                nc.vector.tensor_copy(codes[:], picked_words[:, t : 2 * H : PACK])
+            d_codes.append(codes)
 
         def interleave_w(mt, copy, tag):
-            grouped = keep.tile([P, P, PACK], BF16, name="w_grouped%d" % mt, tag=tag, align_bytes=64)
+            grouped = keep.tile([P, P, PACK], BF16, name="w_grouped%d" % mt, tag=tag, align_bytes=MX_ALIGN)
             cols = slice((mt % 2) * P, (mt % 2 + 1) * P)
             copy(
                 grouped[:].rearrange("p (c i) j -> p c j i", i=4),
-                w_raw[mt // 2][:, :, cols].rearrange("p j (c i) -> p c j i", i=4),
+                w_halves[mt // 2][:, :, cols].rearrange("p j (c i) -> p c j i", i=4),
             )
             return grouped
 
         def quantize_w(mt, grouped, tag):
-            codes = keep.tile([P, P], U32, name="w_codes%d" % mt, tag=tag, align_bytes=64)
-            scales = keep.tile([P, P], U8, name="w_scales%d" % mt, align_bytes=64)
+            codes = keep.tile([P, P], U32, name="w_codes%d" % mt, tag=tag, align_bytes=MX_ALIGN)
+            scales = keep.tile([P, P], U8, name="w_scales%d" % mt, align_bytes=MX_ALIGN)
             nc.vector.quantize_mx(codes[:].bitcast(FP8X4), scales[:], grouped[:].rearrange("p c j -> p (c j)"))
             return codes, scales
 
-        w_early = [interleave_w(mt, nc.scalar.copy, "w_grouped%d" % mt) for mt in range(2)]
+        w_early = [interleave_w(mt, nc.scalar.copy, "w_grouped%d" % mt) for mt in range(EARLY_TILES)]
 
         h_ps = [psum.tile([P, S], F32, name="h_ps%d" % t) for t in range(PACK)]
         for t in range(PACK):
             for li in range(2):
                 nc.tensor.matmul_mx(
                     out=h_ps[t][:],
-                    lhsT=d_mx[t][0][:, li * P : (li + 1) * P].bitcast(FP8X4),
-                    lhsT_scale=d_mx[t][1][:, li * P : (li + 1) * P],
+                    lhsT=d_codes[t][:, li * P : (li + 1) * P].bitcast(FP8X4),
+                    lhsT_scale=d_planes[:, t, li * P : (li + 1) * P],
                     rhs=x_codes[:].bitcast(FP8X4),
-                    rhs_scale=moved[:, 2 * H :],
+                    rhs_scale=placed_bytes[:, 2 * H :],
                     start=(li == 0),
                     stop=(li == 1),
                 )
@@ -124,7 +139,7 @@ def tile_picked_haqratiosend_none_p_kernel(
             nc.scalar.activation(pa[:], h[:].indirect(n1_l[:]), COPY)
             flipped = keep.tile([P, W], F32, name="flipped%d" % t)
             den = keep.tile([P, W], F32, name="den%d" % t)
-            rec = keep.tile([P, W], F32, name="rec%d" % t, align_bytes=64)
+            rec = keep.tile([P, W], F32, name="rec%d" % t, align_bytes=MX_ALIGN)
             ra = keep.tile([P, W], F32, name="ra%d" % t)
             rb = keep.tile([P, W], F32, name="rb%d" % t)
             nc.vector.tensor_scalar(flipped[:], pb[:], -1.0, 0.5, ALU.mult, ALU.add)
@@ -137,22 +152,21 @@ def tile_picked_haqratiosend_none_p_kernel(
             nc.scalar.activation(dt[:].indirect(n1_l[:]), ra[:], COPY)
             dts.append(dt)
 
-        w_mx = [quantize_w(mt, w_early[mt], "rec%d" % mt) for mt in range(2)]
+        w_mx = [quantize_w(mt, w_early[mt], "rec%d" % mt) for mt in range(EARLY_TILES)]
 
-        HALF = S // 2
-        z = keep.tile([P, S, PACK], BF16, tag="rec3", align_bytes=64)
-        for t in range(PACK - 1):
+        last = PACK - 1
+        z = keep.tile([P, S, PACK], BF16, tag="rec%d" % last, align_bytes=MX_ALIGN)
+        for t in range(last):
             nc.vector.tensor_scalar(z[:, :, t], dts[t][:], gain[:, t : t + 1], None, ALU.mult)
-        t = PACK - 1
-        for c0 in (0, HALF):
-            nc.vector.tensor_scalar(z[:, c0 : c0 + HALF, t], dts[t][:, c0 : c0 + HALF], gain[:, t : t + 1], None, ALU.mult)
-        z_codes = keep.tile([P, S], U32, align_bytes=64)
-        z_scales = keep.tile([P, S], U8, align_bytes=64)
-        for c0 in (0, HALF):
+        for c0, width in PIECES:
+            cols = slice(c0, c0 + width)
+            nc.vector.tensor_scalar(z[:, cols, last], dts[last][:, cols], gain[:, last : last + 1], None, ALU.mult)
+        z_codes = keep.tile([P, S], U32, align_bytes=MX_ALIGN)
+        z_scales = keep.tile([P, S], U8, align_bytes=MX_ALIGN)
+        for c0, width in PIECES:
+            cols = slice(c0, c0 + width)
             nc.vector.quantize_mx(
-                z_codes[:, c0 : c0 + HALF].bitcast(FP8X4),
-                z_scales[:, c0 : c0 + HALF],
-                z[:, c0 : c0 + HALF, :].rearrange("p c j -> p (c j)"),
+                z_codes[:, cols].bitcast(FP8X4), z_scales[:, cols], z[:, cols, :].rearrange("p c j -> p (c j)")
             )
 
         def product(mt, c0, width, bank):
@@ -168,27 +182,42 @@ def tile_picked_haqratiosend_none_p_kernel(
             )
             return h2
 
-        def send(mt, c0, h2, sent):
+        def send(mt, c0, h2, ds2):
             width = h2.shape[1]
             rl = keep.tile([P, width], F32, name="rl%d_%d" % (mt, c0))
             nc.vector.tensor_scalar(rl[:], h2[:], 0.0, None, ALU.max)
-            nc.scalar.activation(sent[:].indirect(n3_l[:, c0 // 16 : (c0 + width) // 16]), rl[:], COPY)
+            nc.scalar.activation(ds2[:].indirect(n3_l[:, c0 // LIST_ROWS : (c0 + width) // LIST_ROWS]), rl[:], COPY)
 
-        sents = [keep.tile([P, 2 * S], F32, name="sent%d" % mt) for mt in range(4)]
-        pieces = [[] for mt in range(4)]
-        for c0 in (0, HALF):
-            for mt in range(2):
-                h2 = product(mt, c0, HALF, "h_ps%d" % (2 * mt + c0 // HALF))
-                send(mt, c0, h2, sents[mt])
+        ds2s = [keep.tile([P, S if mt < EARLY_TILES else 2 * S], F32, name="ds2_%d" % mt) for mt in range(OUT_TILES)]
+        pieces = [[] for mt in range(OUT_TILES)]
+        banks = ["h_ps0", "h_ps1", "h_ps2", "h_ps3", "h2_ps0", "h2_ps1"]
+        for piece, (c0, width) in enumerate(PIECES):
+            for mt in range(EARLY_TILES):
+                h2 = product(mt, c0, width, banks[EARLY_TILES * piece + mt])
+                send(mt, c0, h2, ds2s[mt])
                 pieces[mt].append((c0, h2))
-        for mt in range(2, 4):
-            w_mx.append(quantize_w(mt, interleave_w(mt, nc.vector.tensor_copy, "w_scales%d" % (mt - 2)), "d_codes%d" % mt))
+
+        for mt in range(EARLY_TILES, OUT_TILES):
+            grouped = interleave_w(mt, nc.vector.tensor_copy, "w_scales%d" % (mt - EARLY_TILES))
+            w_mx.append(quantize_w(mt, grouped, "d_codes%d" % mt))
             pieces[mt].append((0, product(mt, 0, S, "h2_ps%d" % mt)))
-        for mt in range(2, 4):
-            send(mt, 0, pieces[mt][0][1], sents[mt])
-        for mt in range(4):
-            res = keep.tile([P, S], F32, name="res%d" % mt, tag="d_codes%d" % (mt + 2) if mt < 2 else "res%d" % mt, align_bytes=64)
-            for c0, h2 in pieces[mt]:
-                cols = slice(c0, c0 + h2.shape[1])
-                nc.vector.scalar_tensor_tensor(res[:, cols], h2[:], -0.5, sents[mt][:, cols], ALU.mult, ALU.add)
-            nc.sync.dma_start(out[mt * P : (mt + 1) * P, :], res[:])
+        for mt in range(EARLY_TILES, OUT_TILES):
+            send(mt, 0, pieces[mt][0][1], ds2s[mt])
+
+        for mt in range(OUT_TILES):
+            tag = "d_codes%d" % (mt + EARLY_TILES) if mt < EARLY_TILES else "res%d" % mt
+            res = keep.tile([P, S], F32, name="res%d" % mt, tag=tag, align_bytes=MX_ALIGN)
+            rows = slice(mt * P, (mt + 1) * P)
+            if mt < OUT_TILES - 1:
+                for c0, h2 in pieces[mt]:
+                    cols = slice(c0, c0 + h2.shape[1])
+                    nc.vector.scalar_tensor_tensor(res[:, cols], h2[:], -0.5, ds2s[mt][:, cols], ALU.mult, ALU.add)
+                nc.sync.dma_start(out[rows, :], res[:])
+            else:
+                h2 = pieces[mt][0][1]
+                for c0, queue in ((0, nc.sync), (S // 2, nc.scalar)):
+                    cols = slice(c0, c0 + S // 2)
+                    nc.vector.scalar_tensor_tensor(
+                        res[:, cols], h2[:, cols], -0.5, ds2s[mt][:, cols], ALU.mult, ALU.add
+                    )
+                    queue.dma_start(out[rows, cols], res[:, cols])

@@ -84,17 +84,23 @@ def tile_picked_haqratiosend_none_p_kernel(
         nc.vector.tensor_copy(picked_words[:, H : 2 * H], d_table[:].bitcast(U32).indirect(kb_l[:]))
 
         d_planes = keep.tile([P, PACK, 2 * P], U8, tag="d_table", align_bytes=MX_ALIGN)
-        d_codes = []
-        for t in range(PACK):
-            codes = keep.tile([P, 2 * P], U32, name="d_codes%d" % t, align_bytes=MX_ALIGN)
-            if t == 0:
-                nc.vector.tensor_copy(codes[:, 0:P], picked_words[:, 0:H:PACK])
-                nc.vector.tensor_copy(d_planes[:, t, :], placed_bytes[:, t : 2 * H : PACK])
-                nc.vector.tensor_copy(codes[:, P : 2 * P], picked_words[:, H : 2 * H : PACK])
-            else:
-                nc.vector.tensor_copy(d_planes[:, t, :], placed_bytes[:, t : 2 * H : PACK])
-                nc.vector.tensor_copy(codes[:], picked_words[:, t : 2 * H : PACK])
-            d_codes.append(codes)
+        codes0 = keep.tile([P, 2 * P], U32, align_bytes=MX_ALIGN)
+        codes1 = keep.tile([P, 2 * P], U32, align_bytes=MX_ALIGN)
+        codes23 = keep.tile([P, 2, 2 * P], U32, align_bytes=MX_ALIGN)
+        nc.vector.tensor_copy(codes0[:, 0:P], picked_words[:, 0:H:PACK])
+        nc.vector.tensor_copy(d_planes[:, 0, :], placed_bytes[:, 0 : 2 * H : PACK])
+        nc.vector.tensor_copy(codes0[:, P : 2 * P], picked_words[:, H : 2 * H : PACK])
+        nc.vector.tensor_copy(d_planes[:, 1, :], placed_bytes[:, 1 : 2 * H : PACK])
+        nc.vector.tensor_copy(codes1[:], picked_words[:, 1 : 2 * H : PACK])
+        nc.vector.tensor_copy(
+            d_planes[:, 2:PACK, :].rearrange("p t m -> p m t"),
+            placed_bytes[:, 0 : 2 * H].rearrange("p (m t) -> p m t", t=PACK)[:, :, 2:PACK],
+        )
+        nc.vector.tensor_copy(
+            codes23[:].rearrange("p t m -> p m t"),
+            picked_words[:].rearrange("p (m t) -> p m t", t=PACK)[:, :, 2:PACK],
+        )
+        d_codes = [codes0[:], codes1[:], codes23[:, 0, :], codes23[:, 1, :]]
 
         def interleave_w(mt, copy, tag):
             grouped = keep.tile([P, P, PACK], BF16, name="w_grouped%d" % mt, tag=tag, align_bytes=MX_ALIGN)
@@ -199,13 +205,13 @@ def tile_picked_haqratiosend_none_p_kernel(
 
         for mt in range(EARLY_TILES, OUT_TILES):
             grouped = interleave_w(mt, nc.vector.tensor_copy, "w_scales%d" % (mt - EARLY_TILES))
-            w_mx.append(quantize_w(mt, grouped, "d_codes%d" % mt))
+            w_mx.append(quantize_w(mt, grouped, "w_codes%d" % mt))
             pieces[mt].append((0, product(mt, 0, S, "h2_ps%d" % mt)))
         for mt in range(EARLY_TILES, OUT_TILES):
             send(mt, 0, pieces[mt][0][1], ds2s[mt])
 
         for mt in range(OUT_TILES):
-            tag = "d_codes%d" % (mt + EARLY_TILES) if mt < EARLY_TILES else "res%d" % mt
+            tag = "w_codes%d" % (mt + EARLY_TILES) if mt < EARLY_TILES else "res%d" % mt
             res = keep.tile([P, S], F32, name="res%d" % mt, tag=tag, align_bytes=MX_ALIGN)
             rows = slice(mt * P, (mt + 1) * P)
             if mt < OUT_TILES - 1:

from contextlib import ExitStack

import concourse.mybir as mybir

K, T, S, N, G, H, W = 512, 1024, 256, 512, 2048, 512, 128
FLOPS = 2 * (2 * K * H * S + H * N * S)

F32 = mybir.dt.float32
BF16 = mybir.dt.bfloat16
I32 = mybir.dt.int32
U32 = mybir.dt.uint32
U16 = mybir.dt.uint16
U8 = mybir.dt.uint8
FP8X4 = mybir.dt.float8_e4m3fn_x4
ALU = mybir.AluOpType
COPY = mybir.ActivationFunctionType.Copy

P = 128
PACK = 4
BLOCK_ROWS = 8
QUADRANT = 32
LIST_ROWS = 16
MX_ALIGN = 64
OUT_TILES = N // P
EARLY_TILES = 2
PIECES = ((0, 64), (64, 64), (128, 128))


def tile_picked_haqratiosend_none_p_kernel(
    tc, x_words, x_scales, d_words, d_scales, gn, w1, offs, ka, kb, n1, n2, n3, out
):
    nc = tc.nc
    with ExitStack() as ctx:
        keep = ctx.enter_context(tc.tile_pool(name="keep", bufs=1))
        psum = ctx.enter_context(tc.psum_pool(name="psum", bufs=1))

        def load_list(name, src):
            lst = keep.tile(list(src.shape), U16, name=name)
            nc.sync.dma_start(lst[:], src)
            return lst

        d_bytes = keep.tile([P, G], U8, align_bytes=MX_ALIGN)
        x_bytes = keep.tile([P, T], U8, tag="x_bytes", align_bytes=MX_ALIGN)
        placed_bytes = keep.tile([P, 2 * H + S], U8, align_bytes=MX_ALIGN)
        nc.vector.memset(x_bytes[:].bitcast(I32), 0)
        nc.vector.memset(d_bytes[:].bitcast(I32), 0)
        nc.gpsimd.memset(placed_bytes[:].bitcast(I32), 0)
        offs_l = load_list("offs_l", offs)
        nc.sync.dma_start(x_bytes[0:P:BLOCK_ROWS, :].bitcast(I32), x_scales[0].bitcast(I32))
        ka_l = load_list("ka_l", ka)
        nc.sync.dma_start(d_bytes[0:P:BLOCK_ROWS, :].bitcast(I32), d_scales[0].bitcast(I32))
        kb_l = load_list("kb_l", kb)
        x_table = keep.tile([P, T], I32)
        d_table = keep.tile([P, G], I32, tag="d_table", align_bytes=MX_ALIGN)
        nc.sync.dma_start(x_table[:], x_words[0].rearrange("p n t -> p (n t)").bitcast(I32))
        n2_l = load_list("n2_l", n2)
        n1_l = load_list("n1_l", n1)
        nc.sync.dma_start(d_table[:], d_words[0].rearrange("p n t -> p (n t)").bitcast(I32))
        w_rows = w1.rearrange("(p j) n -> p j n", j=PACK)
        w_first = keep.tile([P, PACK, N // 2], F32)
        nc.sync.dma_start(w_first[:], w_rows[:, :, 0 : N // 2])
        gain = keep.tile([P, PACK], F32)
        nc.scalar.dma_start(gain[:], gn.rearrange("(p j) o -> p (j o)", j=PACK))
        n3_l = load_list("n3_l", n3)

        picked_bytes = keep.tile([P, 2 * H + S], U8, tag="picked_bytes")
        nc.vector.tensor_copy(picked_bytes[:, 2 * H :], x_bytes[:].indirect(offs_l[:]))
        nc.vector.tensor_copy(picked_bytes[:, 0:H], d_bytes[:].indirect(ka_l[:]))
        nc.vector.tensor_copy(picked_bytes[:, H : 2 * H], d_bytes[:].indirect(kb_l[:]))
        for b in range(QUADRANT // BLOCK_ROWS):
            nc.scalar.dma_start(
                placed_bytes[b:P:QUADRANT, :].bitcast(I32),
                picked_bytes[BLOCK_ROWS * b : P : QUADRANT, :].bitcast(I32),
            )

        w_second = keep.tile([P, PACK, N // 2], F32, tag="picked_bytes")
        nc.sync.dma_start(w_second[:], w_rows[:, :, N // 2 : N])
        w_halves = [w_first, w_second]

        x_codes = keep.tile([P, S], U32, align_bytes=MX_ALIGN)
        nc.vector.tensor_copy(x_codes[:], x_table[:].bitcast(U32).indirect(offs_l[:]))
        picked_words = keep.tile([P, 2 * H], U32, tag="x_bytes", align_bytes=MX_ALIGN)
        nc.vector.tensor_copy(picked_words[:, 0:H], d_table[:].bitcast(U32).indirect(ka_l[:]))
        nc.vector.tensor_copy(picked_words[:, H : 2 * H], d_table[:].bitcast(U32).indirect(kb_l[:]))

        d_planes = keep.tile([P, PACK, 2 * P], U8, tag="d_table", align_bytes=MX_ALIGN)
        codes0 = keep.tile([P, 2 * P], U32, align_bytes=MX_ALIGN)
        codes1 = keep.tile([P, 2 * P], U32, align_bytes=MX_ALIGN)
        codes23 = keep.tile([P, 2, 2 * P], U32, align_bytes=MX_ALIGN)
        nc.vector.tensor_copy(codes0[:, 0:P], picked_words[:, 0:H:PACK])
        nc.vector.tensor_copy(d_planes[:, 0, :], placed_bytes[:, 0 : 2 * H : PACK])
        nc.vector.tensor_copy(codes0[:, P : 2 * P], picked_words[:, H : 2 * H : PACK])
        nc.vector.tensor_copy(d_planes[:, 1, :], placed_bytes[:, 1 : 2 * H : PACK])
        nc.vector.tensor_copy(codes1[:], picked_words[:, 1 : 2 * H : PACK])
        nc.vector.tensor_copy(
            d_planes[:, 2:PACK, :].rearrange("p t m -> p m t"),
            placed_bytes[:, 0 : 2 * H].rearrange("p (m t) -> p m t", t=PACK)[:, :, 2:PACK],
        )
        nc.vector.tensor_copy(
            codes23[:].rearrange("p t m -> p m t"),
            picked_words[:].rearrange("p (m t) -> p m t", t=PACK)[:, :, 2:PACK],
        )
        d_codes = [codes0[:], codes1[:], codes23[:, 0, :], codes23[:, 1, :]]

        def interleave_w(mt, copy, tag):
            grouped = keep.tile([P, P, PACK], BF16, name="w_grouped%d" % mt, tag=tag, align_bytes=MX_ALIGN)
            cols = slice((mt % 2) * P, (mt % 2 + 1) * P)
            copy(
                grouped[:].rearrange("p (c i) j -> p c j i", i=4),
                w_halves[mt // 2][:, :, cols].rearrange("p j (c i) -> p c j i", i=4),
            )
            return grouped

        def quantize_w(mt, grouped, tag):
            codes = keep.tile([P, P], U32, name="w_codes%d" % mt, tag=tag, align_bytes=MX_ALIGN)
            scales = keep.tile([P, P], U8, name="w_scales%d" % mt, align_bytes=MX_ALIGN)
            nc.vector.quantize_mx(codes[:].bitcast(FP8X4), scales[:], grouped[:].rearrange("p c j -> p (c j)"))
            return codes, scales

        w_early = [interleave_w(mt, nc.scalar.copy, "w_grouped%d" % mt) for mt in range(EARLY_TILES)]

        h_ps = [psum.tile([P, S], F32, name="h_ps%d" % t) for t in range(PACK)]
        for t in range(PACK):
            for li in range(2):
                nc.tensor.matmul_mx(
                    out=h_ps[t][:],
                    lhsT=d_codes[t][:, li * P : (li + 1) * P].bitcast(FP8X4),
                    lhsT_scale=d_planes[:, t, li * P : (li + 1) * P],
                    rhs=x_codes[:].bitcast(FP8X4),
                    rhs_scale=placed_bytes[:, 2 * H :],
                    start=(li == 0),
                    stop=(li == 1),
                )

        dts = []
        for t in range(PACK):
            h = keep.tile([P, S], F32, name="h%d" % t)
            if t == 0:
                nc.scalar.activation(h[:], h_ps[t][:], COPY, scale=0.0625)
            else:
                nc.vector.tensor_scalar(h[:], h_ps[t][:], 0.0625, None, ALU.mult)
            pa = keep.tile([P, W], F32, name="pa%d" % t)
            pb = keep.tile([P, W], F32, name="pb%d" % t)
            nc.scalar.activation(pb[:], h[:].indirect(n2_l[:]), COPY)
            nc.scalar.activation(pa[:], h[:].indirect(n1_l[:]), COPY)
            flipped = keep.tile([P, W], F32, name="flipped%d" % t)
            den = keep.tile([P, W], F32, name="den%d" % t)
            rec = keep.tile([P, W], F32, name="rec%d" % t, align_bytes=MX_ALIGN)
            ra = keep.tile([P, W], F32, name="ra%d" % t)
            rb = keep.tile([P, W], F32, name="rb%d" % t)
            nc.vector.tensor_scalar(flipped[:], pb[:], -1.0, 0.5, ALU.mult, ALU.add)
            nc.vector.tensor_tensor(rb[:], pa[:], pb[:], ALU.max)
            nc.vector.scalar_tensor_tensor(den[:], pb[:], 0.5, flipped[:], ALU.add, ALU.max)
            nc.vector.reciprocal(rec[:], den[:])
            nc.vector.tensor_tensor(ra[:], pa[:], rec[:], ALU.mult)
            dt = keep.tile([P, S], F32, name="dt%d" % t)
            nc.scalar.activation(dt[:].indirect(n2_l[:]), rb[:], COPY)
            nc.scalar.activation(dt[:].indirect(n1_l[:]), ra[:], COPY)
            dts.append(dt)

        w_mx = [quantize_w(mt, w_early[mt], "rec%d" % mt) for mt in range(EARLY_TILES)]

        last = PACK - 1
        z = keep.tile([P, S, PACK], BF16, tag="rec%d" % last, align_bytes=MX_ALIGN)
        for t in range(last):
            nc.vector.tensor_scalar(z[:, :, t], dts[t][:], gain[:, t : t + 1], None, ALU.mult)
        for c0, width in PIECES:
            cols = slice(c0, c0 + width)
            nc.vector.tensor_scalar(z[:, cols, last], dts[last][:, cols], gain[:, last : last + 1], None, ALU.mult)
        z_codes = keep.tile([P, S], U32, align_bytes=MX_ALIGN)
        z_scales = keep.tile([P, S], U8, align_bytes=MX_ALIGN)
        for c0, width in PIECES:
            cols = slice(c0, c0 + width)
            nc.vector.quantize_mx(
                z_codes[:, cols].bitcast(FP8X4), z_scales[:, cols], z[:, cols, :].rearrange("p c j -> p (c j)")
            )

        def product(mt, c0, width, bank):
            h2 = psum.tile([P, width], F32, name="h2_ps%d_%d" % (mt, c0), tag=bank)
            nc.tensor.matmul_mx(
                out=h2[:],
                lhsT=w_mx[mt][0][:].bitcast(FP8X4),
                lhsT_scale=w_mx[mt][1][:],
                rhs=z_codes[:, c0 : c0 + width].bitcast(FP8X4),
                rhs_scale=z_scales[:, c0 : c0 + width],
                start=True,
                stop=True,
            )
            return h2

        def send(mt, c0, h2, ds2):
            width = h2.shape[1]
            rl = keep.tile([P, width], F32, name="rl%d_%d" % (mt, c0))
            nc.vector.tensor_scalar(rl[:], h2[:], 0.0, None, ALU.max)
            nc.scalar.activation(ds2[:].indirect(n3_l[:, c0 // LIST_ROWS : (c0 + width) // LIST_ROWS]), rl[:], COPY)

        ds2s = [keep.tile([P, S if mt < EARLY_TILES else 2 * S], F32, name="ds2_%d" % mt) for mt in range(OUT_TILES)]
        pieces = [[] for mt in range(OUT_TILES)]
        banks = ["h_ps0", "h_ps1", "h_ps2", "h_ps3", "h2_ps0", "h2_ps1"]
        for piece, (c0, width) in enumerate(PIECES):
            for mt in range(EARLY_TILES):
                h2 = product(mt, c0, width, banks[EARLY_TILES * piece + mt])
                send(mt, c0, h2, ds2s[mt])
                pieces[mt].append((c0, h2))

        for mt in range(EARLY_TILES, OUT_TILES):
            grouped = interleave_w(mt, nc.vector.tensor_copy, "w_scales%d" % (mt - EARLY_TILES))
            w_mx.append(quantize_w(mt, grouped, "w_codes%d" % mt))
            pieces[mt].append((0, product(mt, 0, S, "h2_ps%d" % mt)))
        for mt in range(EARLY_TILES, OUT_TILES):
            send(mt, 0, pieces[mt][0][1], ds2s[mt])

        for mt in range(OUT_TILES):
            tag = "w_codes%d" % (mt + EARLY_TILES) if mt < EARLY_TILES else "res%d" % mt
            res = keep.tile([P, S], F32, name="res%d" % mt, tag=tag, align_bytes=MX_ALIGN)
            rows = slice(mt * P, (mt + 1) * P)
            if mt < OUT_TILES - 1:
                for c0, h2 in pieces[mt]:
                    cols = slice(c0, c0 + h2.shape[1])
                    nc.vector.scalar_tensor_tensor(res[:, cols], h2[:], -0.5, ds2s[mt][:, cols], ALU.mult, ALU.add)
                nc.sync.dma_start(out[rows, :], res[:])
            else:
                h2 = pieces[mt][0][1]
                for c0, queue in ((0, nc.sync), (S // 2, nc.scalar)):
                    cols = slice(c0, c0 + S // 2)
                    nc.vector.scalar_tensor_tensor(
                        res[:, cols], h2[:, cols], -0.5, ds2s[mt][:, cols], ALU.mult, ALU.add
                    )
                    queue.dma_start(out[rows, cols], res[:, cols])
